import numpy as np
import ml_dtypes


def mxq(x, axis, fmt="e4m3"):
    dtype, down = {"e4m3": (ml_dtypes.float8_e4m3fn, 7), "e5m2": (ml_dtypes.float8_e5m2, 14)}[fmt]
    v = np.moveaxis(np.asarray(x, np.float32).astype(ml_dtypes.bfloat16).astype(np.float64), axis, -1)
    blocks = v.reshape(v.shape[:-1] + (-1, 32))
    amax = np.abs(blocks).max(-1, keepdims=True)
    byte = np.maximum(np.where(amax > 0, np.frexp(amax)[1] - 1 + 127, 0) - down, 1)
    scale = np.exp2(byte - 127.0)
    codes = (blocks / scale).astype(np.float32).astype(dtype).astype(np.float64)
    return np.moveaxis((codes * scale).reshape(v.shape), -1, axis)


WIDE = False


def mx_kscale(k):
    if not WIDE:
        return np.ones(k)
    levels = np.array([10, -10, 5, -5, 0])
    if k % 512:
        return np.exp2(np.random.permutation(np.resize(levels, k // 32))).repeat(32)
    a = np.empty((k // 512, 16))
    for p in range(k // 512):
        a[p, :8] = np.random.permutation(np.resize(levels, 8))
        for g in range(8):
            far = levels[np.abs(levels - a[p, g]) >= 10]
            a[p, g + 8] = far[np.random.randint(len(far))]
    return np.exp2(a.ravel()).repeat(32)


def f64(x):
    return np.asarray(x).astype(np.float64)


def striped(idx):
    return np.tile(np.asarray(idx).reshape(-1, 16).T, (8, 1)).astype(np.uint16)


def unstriped(offs):
    return offs[:16].T.reshape(-1).astype(np.int64)


E2M1 = np.array([0.0, 0.5, 1.0, 1.5, 2.0, 3.0, 4.0, 6.0, -0.0, -0.5, -1.0, -1.5, -2.0, -3.0, -4.0, -6.0])


def pack_weight(w, fmt):
    k, n = w.shape
    w = f64(np.asarray(w, np.float32).astype(ml_dtypes.bfloat16)).reshape(k // 32, 32, n)
    amax = np.abs(w).max(1)
    if fmt == "e4m3":
        byte = np.frexp(amax)[1] - 1 + 127 - 7
    else:
        mant, ex = np.frexp(amax / 6.0)
        byte = np.where(mant > 0.5, ex, ex - 1) + 127
    byte = np.clip(np.where(amax > 0, byte, 1), 1, 254)
    scaled = (w * np.exp2(127.0 - byte)[:, None, :]).reshape(k, n).astype(np.float32)
    by_word = np.ascontiguousarray(scaled.reshape(k // 512, 128, 4, n).transpose(0, 1, 3, 2))
    if fmt == "e4m3":
        words = by_word.astype(ml_dtypes.float8_e4m3fn).view(np.uint8)
    else:
        c = by_word.astype(ml_dtypes.float4_e2m1fn).view(np.uint8) & 0xF
        words = (c[..., 0::2] | (c[..., 1::2] << 4)).reshape(k // 512, 128, 2 * n)
    return np.ascontiguousarray(words), np.ascontiguousarray(byte.astype(np.uint8).reshape(k // 512, 16, n))


def unpack_weight(words, scales, fmt):
    g, _, n = scales.shape
    words = np.ascontiguousarray(words).reshape(g, 128, n, -1)
    if fmt == "e4m3":
        vals = words.view(ml_dtypes.float8_e4m3fn).astype(np.float64)
    else:
        nib = np.empty((g, 128, n, 4), np.uint8)
        nib[..., 0::2] = words & 0xF
        nib[..., 1::2] = words >> 4
        vals = E2M1[nib]
    vals = vals * np.repeat(np.exp2(scales.astype(np.float64) - 127.0), 8, axis=1)[..., None]
    return vals.transpose(0, 1, 3, 2).reshape(g * 512, n)


B, N, T, D, NQ = 1, 1024, 4096, 512, 128
SEG = 32


def setup_inputs():
    n = np.random.standard_normal
    pages = np.random.permutation(T // 32)[:B * N // 32]
    idx = (pages[:, None] * 32 + np.arange(32)[None, :]).reshape(-1)
    s = mx_kscale(D)[:, None]
    kp = pack_weight(n((D, T)) / s, "e4m3")
    return {
        "qT": (n((B, D, NQ)) * s * (1.00 / np.sqrt(D))).astype(np.float32),
        "k_words": kp[0],
        "k_scales": kp[1],
        "th": (n((B, NQ, 1)) + 1).astype(np.float32),
        "offs": striped(idx),
    }


def reference(qT, k_words, k_scales, th, offs):
    idx = unstriped(offs)
    pick = lambda x, which: x[:, which].reshape(x.shape[0], B, -1).transpose(1, 0, 2)
    k = unpack_weight(k_words, k_scales, "e4m3")
    kg = pick(k, idx)
    qq = mxq(f64(qT), 1, "e4m3")
    a = qq.transpose(0, 2, 1) @ kg
    x = np.maximum(a.reshape(B, NQ, N // SEG, SEG).max(-1) - f64(th), 0.0)
    y = x / (1.0 + x)
    return y

@@ -1,0 +1,101 @@
+from contextlib import ExitStack
+
+import concourse.mybir as mybir
+
+F32 = mybir.dt.float32
+BF16 = mybir.dt.bfloat16
+I32 = mybir.dt.int32
+U32 = mybir.dt.uint32
+U16 = mybir.dt.uint16
+U8 = mybir.dt.uint8
+FP8X4 = mybir.dt.float8_e4m3fn_x4
+ALU = mybir.AluOpType
+
+P = 128
+PACK = 4
+T = 4096
+N = 1024
+NQ = 128
+SEG = 32
+GATHER = 512
+MM = 256
+
+FLOPS = 2 * 512 * NQ * N
+
+
+def tile_attend_page_margin_kernel(tc, qT, k_words, k_scales, th, offs, out):
+    nc = tc.nc
+    with ExitStack() as ctx:
+        pool = ctx.enter_context(tc.tile_pool(name="held", bufs=1))
+        psum = ctx.enter_context(tc.psum_pool(name="psum", bufs=1))
+
+        offsets = pool.tile([P, N // 16], U16, name="offsets")
+        nc.sync.dma_start(offsets[:], offs)
+
+        words = pool.tile([P, T], I32, name="words", align_bytes=64)
+        nc.sync.dma_start(out=words[:], in_=k_words[0].rearrange("p n t -> p (n t)").bitcast(I32))
+
+        scales = pool.tile([P, T // 4], I32, name="scales", align_bytes=64)
+        nc.vector.memset(scales[:], 0)
+
+        q_raw = pool.tile([P, PACK, NQ], F32, name="q_raw")
+        nc.scalar.dma_start(out=q_raw[:], in_=qT[0].rearrange("(p j) w -> p j w", j=PACK))
+        for quad in range(4):
+            nc.scalar.dma_start(
+                out=scales[32 * quad : 32 * quad + 4, :],
+                in_=k_scales[0][4 * quad : 4 * quad + 4, :].bitcast(I32),
+            )
+        thr = pool.tile([P, 1], F32, name="thr")
+        nc.scalar.dma_start(out=thr[:], in_=th[0])
+
+        q_bf = pool.tile([P, NQ, PACK], BF16, name="q_bf", align_bytes=64)
+        nc.vector.tensor_copy(out=q_bf[:], in_=q_raw[:].rearrange("p j w -> p w j"))
+        q_codes = pool.tile([P, NQ], U32, name="q_codes", align_bytes=64)
+        q_scales = pool.tile([P, NQ], U8, name="q_scales", align_bytes=64)
+
+        one_less_thr = pool.tile([P, 1], F32, name="one_less_thr")
+        nc.vector.tensor_scalar(out=one_less_thr[:], in0=thr[:], scalar1=-1.0, scalar2=1.0, op0=ALU.mult, op1=ALU.add)
+
+        nc.vector.quantize_mx(
+            out=q_codes[:].bitcast(FP8X4), scales=q_scales[:], in_=q_bf[:].rearrange("p w j -> p (w j)")
+        )
+
+        key_scales = pool.tile([P, N], U8, name="key_scales", align_bytes=64)
+        nc.vector.tensor_copy(out=key_scales[:], in_=scales[:].bitcast(U8).indirect(offsets[:]))
+
+        key_words = []
+        for h in range(N // GATHER):
+            kw = pool.tile([P, GATHER], U32, name=f"key_words{h}", align_bytes=64)
+            cols = slice(h * GATHER // 16, (h + 1) * GATHER // 16)
+            nc.vector.tensor_copy(out=kw[:], in_=words[:].bitcast(U32).indirect(offsets[:, cols]))
+            key_words.append(kw)
+
+        best = pool.tile([P, N // SEG], F32, name="best")
+        for m in range(N // MM):
+            h, c0 = divmod(m * MM, GATHER)
+            scores = psum.tile([P, 512], F32, name=f"scores{m}")
+            nc.tensor.matmul_mx(
+                out=scores[:, 0:MM],
+                lhsT=q_codes[:].bitcast(FP8X4),
+                lhsT_scale=q_scales[:],
+                rhs=key_words[h][:, c0 : c0 + MM].bitcast(FP8X4),
+                rhs_scale=key_scales[:, m * MM : (m + 1) * MM],
+                start=True,
+                stop=True,
+            )
+            nc.vector.tensor_reduce(
+                out=best[:, m * MM // SEG : (m + 1) * MM // SEG],
+                in_=scores[:, 0:MM].rearrange("p (j s) -> p j s", s=SEG),
+                axis=mybir.AxisListType.X,
+                op=ALU.max,
+            )
+
+        denom = pool.tile([P, N // SEG], F32, name="denom")
+        nc.vector.tensor_scalar(out=denom[:], in0=best[:], scalar1=one_less_thr[:], scalar2=1.0, op0=ALU.add, op1=ALU.max)
+        margin = pool.tile([P, N // SEG], F32, name="margin")
+        nc.vector.tensor_scalar(out=margin[:], in0=best[:], scalar1=thr[:], scalar2=0.0, op0=ALU.subtract, op1=ALU.max)
+        inv = pool.tile([P, N // SEG], F32, name="inv")
+        nc.vector.reciprocal(out=inv[:], in_=denom[:])
+        res = pool.tile([P, N // SEG], F32, name="res")
+        nc.vector.tensor_tensor(out=res[:], in0=margin[:], in1=inv[:], op=ALU.mult)
+        nc.sync.dma_start(out=out[0], in_=res[:])

@@ -32,21 +32,27 @@ def tile_attend_page_margin_kernel(tc, qT, k_words, k_scales, th, offs, out):
         offsets = pool.tile([P, N // 16], U16, name="offsets")
         nc.sync.dma_start(offsets[:], offs)
 
+        q_raw = pool.tile([P, PACK, NQ], F32, name="q_raw")
+        nc.sync.dma_start(out=q_raw[:], in_=qT[0].rearrange("(p j) w -> p j w", j=PACK))
+
         words = pool.tile([P, T], I32, name="words", align_bytes=64)
-        nc.sync.dma_start(out=words[:], in_=k_words[0].rearrange("p n t -> p (n t)").bitcast(I32))
+        nc.sync.dma_start(
+            out=words[:], in_=k_words[0].rearrange("p n t -> p (n t)").bitcast(I32), max_dma_last_dim=8192
+        )
 
         scales = pool.tile([P, T // 4], I32, name="scales", align_bytes=64)
         nc.vector.memset(scales[:], 0)
+        key_scales = pool.tile([P, N // 4], I32, name="key_scales", align_bytes=64)
+        nc.vector.memset(key_scales[:], 0)
 
-        q_raw = pool.tile([P, PACK, NQ], F32, name="q_raw")
-        nc.scalar.dma_start(out=q_raw[:], in_=qT[0].rearrange("(p j) w -> p j w", j=PACK))
-        for quad in range(4):
-            nc.scalar.dma_start(
-                out=scales[32 * quad : 32 * quad + 4, :],
-                in_=k_scales[0][4 * quad : 4 * quad + 4, :].bitcast(I32),
-            )
+        nc.scalar.dma_start(out=scales[0:P:8, :], in_=k_scales[0].bitcast(I32))
         thr = pool.tile([P, 1], F32, name="thr")
         nc.scalar.dma_start(out=thr[:], in_=th[0])
+
+        picked = pool.tile([P, N], U8, name="picked", align_bytes=64)
+        nc.vector.tensor_copy(out=picked[:], in_=scales[:].bitcast(U8).indirect(offsets[:]))
+        for r in range(4):
+            nc.scalar.dma_start(out=key_scales[r:P:32, :], in_=picked[8 * r : P : 32, :].bitcast(I32))
 
         q_bf = pool.tile([P, NQ, PACK], BF16, name="q_bf", align_bytes=64)
         nc.vector.tensor_copy(out=q_bf[:], in_=q_raw[:].rearrange("p j w -> p w j"))
@@ -59,9 +65,6 @@ def tile_attend_page_margin_kernel(tc, qT, k_words, k_scales, th, offs, out):
         nc.vector.quantize_mx(
             out=q_codes[:].bitcast(FP8X4), scales=q_scales[:], in_=q_bf[:].rearrange("p w j -> p (w j)")
         )
-
-        key_scales = pool.tile([P, N], U8, name="key_scales", align_bytes=64)
-        nc.vector.tensor_copy(out=key_scales[:], in_=scales[:].bitcast(U8).indirect(offsets[:]))
 
         key_words = []
         for h in range(N // GATHER):
@@ -79,7 +82,7 @@ def tile_attend_page_margin_kernel(tc, qT, k_words, k_scales, th, offs, out):
                 lhsT=q_codes[:].bitcast(FP8X4),
                 lhsT_scale=q_scales[:],
                 rhs=key_words[h][:, c0 : c0 + MM].bitcast(FP8X4),
-                rhs_scale=key_scales[:, m * MM : (m + 1) * MM],
+                rhs_scale=key_scales[:].bitcast(U8)[:, m * MM : (m + 1) * MM],
                 start=True,
                 stop=True,
             )

@@ -33,34 +33,30 @@ def tile_attend_page_margin_kernel(tc, qT, k_words, k_scales, th, offs, out):
         nc.sync.dma_start(offsets[:], offs)
 
         q_raw = pool.tile([P, PACK, NQ], F32, name="q_raw")
-        nc.sync.dma_start(out=q_raw[:], in_=qT[0].rearrange("(p j) w -> p j w", j=PACK))
-
-        words = pool.tile([P, T], I32, name="words", align_bytes=64)
-        nc.sync.dma_start(
-            out=words[:], in_=k_words[0].rearrange("p n t -> p (n t)").bitcast(I32), max_dma_last_dim=8192
-        )
+        nc.scalar.dma_start(out=q_raw[:], in_=qT[0].rearrange("(p j) w -> p j w", j=PACK))
 
         scales = pool.tile([P, T // 4], I32, name="scales", align_bytes=64)
         nc.vector.memset(scales[:], 0)
         key_scales = pool.tile([P, N // 4], I32, name="key_scales", align_bytes=64)
         nc.vector.memset(key_scales[:], 0)
+        nc.sync.dma_start(out=scales[0:P:8, :], in_=k_scales[0].bitcast(I32))
 
-        nc.scalar.dma_start(out=scales[0:P:8, :], in_=k_scales[0].bitcast(I32))
+        words = pool.tile([P, T], I32, name="words", align_bytes=64)
+        nc.scalar.dma_start(
+            out=words[:], in_=k_words[0].rearrange("p n t -> p (n t)").bitcast(I32), max_dma_last_dim=8192
+        )
         thr = pool.tile([P, 1], F32, name="thr")
         nc.scalar.dma_start(out=thr[:], in_=th[0])
 
         picked = pool.tile([P, N], U8, name="picked", align_bytes=64)
         nc.vector.tensor_copy(out=picked[:], in_=scales[:].bitcast(U8).indirect(offsets[:]))
         for r in range(4):
-            nc.scalar.dma_start(out=key_scales[r:P:32, :], in_=picked[8 * r : P : 32, :].bitcast(I32))
+            nc.sync.dma_start(out=key_scales[r:P:32, :], in_=picked[8 * r : P : 32, :].bitcast(I32))
 
         q_bf = pool.tile([P, NQ, PACK], BF16, name="q_bf", align_bytes=64)
         nc.vector.tensor_copy(out=q_bf[:], in_=q_raw[:].rearrange("p j w -> p w j"))
         q_codes = pool.tile([P, NQ], U32, name="q_codes", align_bytes=64)
         q_scales = pool.tile([P, NQ], U8, name="q_scales", align_bytes=64)
-
-        one_less_thr = pool.tile([P, 1], F32, name="one_less_thr")
-        nc.vector.tensor_scalar(out=one_less_thr[:], in0=thr[:], scalar1=-1.0, scalar2=1.0, op0=ALU.mult, op1=ALU.add)
 
         nc.vector.quantize_mx(
             out=q_codes[:].bitcast(FP8X4), scales=q_scales[:], in_=q_bf[:].rearrange("p w j -> p (w j)")
@@ -72,6 +68,9 @@ def tile_attend_page_margin_kernel(tc, qT, k_words, k_scales, th, offs, out):
             cols = slice(h * GATHER // 16, (h + 1) * GATHER // 16)
             nc.vector.tensor_copy(out=kw[:], in_=words[:].bitcast(U32).indirect(offsets[:, cols]))
             key_words.append(kw)
+
+        one_less_thr = pool.tile([P, 1], F32, name="one_less_thr")
+        nc.vector.tensor_scalar(out=one_less_thr[:], in0=thr[:], scalar1=-1.0, scalar2=1.0, op0=ALU.mult, op1=ALU.add)
 
         best = pool.tile([P, N // SEG], F32, name="best")
         for m in range(N // MM):

@@ -39,7 +39,7 @@ def tile_attend_page_margin_kernel(tc, qT, k_words, k_scales, th, offs, out):
         nc.vector.memset(scales[:], 0)
         key_scales = pool.tile([P, N // 4], I32, name="key_scales", align_bytes=64)
         nc.vector.memset(key_scales[:], 0)
-        nc.sync.dma_start(out=scales[0:P:8, :], in_=k_scales[0].bitcast(I32))
+        nc.sync.dma_start(out=scales[4:P:8, :], in_=k_scales[0].bitcast(I32))
 
         words = pool.tile([P, T], I32, name="words", align_bytes=64)
         nc.scalar.dma_start(
@@ -51,7 +51,7 @@ def tile_attend_page_margin_kernel(tc, qT, k_words, k_scales, th, offs, out):
         picked = pool.tile([P, N], U8, name="picked", align_bytes=64)
         nc.vector.tensor_copy(out=picked[:], in_=scales[:].bitcast(U8).indirect(offsets[:]))
         for r in range(4):
-            nc.sync.dma_start(out=key_scales[r:P:32, :], in_=picked[8 * r : P : 32, :].bitcast(I32))
+            nc.sync.dma_start(out=key_scales[r:P:32, :], in_=picked[8 * r + 4 : P : 32, :].bitcast(I32))
 
         q_bf = pool.tile([P, NQ, PACK], BF16, name="q_bf", align_bytes=64)
         nc.vector.tensor_copy(out=q_bf[:], in_=q_raw[:].rearrange("p j w -> p w j"))
@@ -93,11 +93,15 @@ def tile_attend_page_margin_kernel(tc, qT, k_words, k_scales, th, offs, out):
             )
 
         denom = pool.tile([P, N // SEG], F32, name="denom")
-        nc.vector.tensor_scalar(out=denom[:], in0=best[:], scalar1=one_less_thr[:], scalar2=1.0, op0=ALU.add, op1=ALU.max)
         margin = pool.tile([P, N // SEG], F32, name="margin")
-        nc.vector.tensor_scalar(out=margin[:], in0=best[:], scalar1=thr[:], scalar2=0.0, op0=ALU.subtract, op1=ALU.max)
         inv = pool.tile([P, N // SEG], F32, name="inv")
-        nc.vector.reciprocal(out=inv[:], in_=denom[:])
         res = pool.tile([P, N // SEG], F32, name="res")
-        nc.vector.tensor_tensor(out=res[:], in0=margin[:], in1=inv[:], op=ALU.mult)
+        parts = (slice(0, 24), slice(24, 32))
+        for c in parts:
+            nc.vector.tensor_scalar(out=denom[:, c], in0=best[:, c], scalar1=one_less_thr[:], scalar2=1.0, op0=ALU.add, op1=ALU.max)
+            nc.vector.tensor_scalar(out=margin[:, c], in0=best[:, c], scalar1=thr[:], scalar2=0.0, op0=ALU.subtract, op1=ALU.max)
+        for c in parts:
+            nc.vector.reciprocal(out=inv[:, c], in_=denom[:, c])
+        for c in parts:
+            nc.vector.tensor_tensor(out=res[:, c], in0=margin[:, c], in1=inv[:, c], op=ALU.mult)
         nc.sync.dma_start(out=out[0], in_=res[:])

@@ -43,7 +43,7 @@ def tile_attend_page_margin_kernel(tc, qT, k_words, k_scales, th, offs, out):
 
         words = pool.tile([P, T], I32, name="words", align_bytes=64)
         nc.scalar.dma_start(
-            out=words[:], in_=k_words[0].rearrange("p n t -> p (n t)").bitcast(I32), max_dma_last_dim=8192
+            out=words[:], in_=k_words[0].rearrange("p n t -> p (n t)").bitcast(I32), max_dma_last_dim=4096
         )
         thr = pool.tile([P, 1], F32, name="thr")
         nc.scalar.dma_start(out=thr[:], in_=th[0])

@@ -32,9 +32,6 @@ def tile_attend_page_margin_kernel(tc, qT, k_words, k_scales, th, offs, out):
         offsets = pool.tile([P, N // 16], U16, name="offsets")
         nc.sync.dma_start(offsets[:], offs)
 
-        q_raw = pool.tile([P, PACK, NQ], F32, name="q_raw")
-        nc.scalar.dma_start(out=q_raw[:], in_=qT[0].rearrange("(p j) w -> p j w", j=PACK))
-
         scales = pool.tile([P, T // 4], I32, name="scales", align_bytes=64)
         nc.vector.memset(scales[:], 0)
         key_scales = pool.tile([P, N // 4], I32, name="key_scales", align_bytes=64)
@@ -42,9 +39,10 @@ def tile_attend_page_margin_kernel(tc, qT, k_words, k_scales, th, offs, out):
         nc.sync.dma_start(out=scales[4:P:8, :], in_=k_scales[0].bitcast(I32))
 
         words = pool.tile([P, T], I32, name="words", align_bytes=64)
-        nc.scalar.dma_start(
-            out=words[:], in_=k_words[0].rearrange("p n t -> p (n t)").bitcast(I32), max_dma_last_dim=4096
-        )
+        words_hbm = k_words[0].rearrange("p n t -> p (n t)").bitcast(I32)
+        nc.scalar.dma_start(out=words[:], in_=words_hbm, max_dma_last_dim=4096)
+        q_raw = pool.tile([P, PACK, NQ], F32, name="q_raw")
+        nc.scalar.dma_start(out=q_raw[:], in_=qT[0].rearrange("(p j) w -> p j w", j=PACK))
         thr = pool.tile([P, 1], F32, name="thr")
         nc.scalar.dma_start(out=thr[:], in_=th[0])
 
@@ -53,21 +51,22 @@ def tile_attend_page_margin_kernel(tc, qT, k_words, k_scales, th, offs, out):
         for r in range(4):
             nc.sync.dma_start(out=key_scales[r:P:32, :], in_=picked[8 * r + 4 : P : 32, :].bitcast(I32))
 
-        q_bf = pool.tile([P, NQ, PACK], BF16, name="q_bf", align_bytes=64)
-        nc.vector.tensor_copy(out=q_bf[:], in_=q_raw[:].rearrange("p j w -> p w j"))
+        q_bf = pool.tile([P, NQ, PACK], BF16, name="q_bf", tag="q_bf_then_keys", align_bytes=64)
+        nc.scalar.copy(out=q_bf[:], in_=q_raw[:].rearrange("p j w -> p w j"))
         q_codes = pool.tile([P, NQ], U32, name="q_codes", align_bytes=64)
         q_scales = pool.tile([P, NQ], U8, name="q_scales", align_bytes=64)
 
-        nc.vector.quantize_mx(
-            out=q_codes[:].bitcast(FP8X4), scales=q_scales[:], in_=q_bf[:].rearrange("p w j -> p (w j)")
-        )
-
         key_words = []
         for h in range(N // GATHER):
-            kw = pool.tile([P, GATHER], U32, name=f"key_words{h}", align_bytes=64)
+            tag = "q_bf_then_keys" if h == 1 else "first_keys"
+            kw = pool.tile([P, GATHER], U32, name=f"key_words{h}", tag=tag, align_bytes=64)
             cols = slice(h * GATHER // 16, (h + 1) * GATHER // 16)
             nc.vector.tensor_copy(out=kw[:], in_=words[:].bitcast(U32).indirect(offsets[:, cols]))
             key_words.append(kw)
+            if h == 0:
+                nc.vector.quantize_mx(
+                    out=q_codes[:].bitcast(FP8X4), scales=q_scales[:], in_=q_bf[:].rearrange("p w j -> p (w j)")
+                )
 
         one_less_thr = pool.tile([P, 1], F32, name="one_less_thr")
         nc.vector.tensor_scalar(out=one_less_thr[:], in0=thr[:], scalar1=-1.0, scalar2=1.0, op0=ALU.mult, op1=ALU.add)

@@ -10,6 +10,7 @@ U16 = mybir.dt.uint16
 U8 = mybir.dt.uint8
 FP8X4 = mybir.dt.float8_e4m3fn_x4
 ALU = mybir.AluOpType
+ACT = mybir.ActivationFunctionType
 
 P = 128
 PACK = 4
@@ -41,7 +42,7 @@ def tile_attend_page_margin_kernel(tc, qT, k_words, k_scales, th, offs, out):
         words = pool.tile([P, T], I32, name="words", align_bytes=64)
         words_hbm = k_words[0].rearrange("p n t -> p (n t)").bitcast(I32)
         nc.scalar.dma_start(out=words[:], in_=words_hbm, max_dma_last_dim=4096)
-        q_raw = pool.tile([P, PACK, NQ], F32, name="q_raw")
+        q_raw = pool.tile([P, PACK, NQ], F32, name="q_raw", tag="q_raw_then_keys", align_bytes=64)
         nc.scalar.dma_start(out=q_raw[:], in_=qT[0].rearrange("(p j) w -> p j w", j=PACK))
         thr = pool.tile([P, 1], F32, name="thr")
         nc.scalar.dma_start(out=thr[:], in_=th[0])
@@ -51,14 +52,16 @@ def tile_attend_page_margin_kernel(tc, qT, k_words, k_scales, th, offs, out):
         for r in range(4):
             nc.sync.dma_start(out=key_scales[r:P:32, :], in_=picked[8 * r + 4 : P : 32, :].bitcast(I32))
 
-        q_bf = pool.tile([P, NQ, PACK], BF16, name="q_bf", tag="q_bf_then_keys", align_bytes=64)
-        nc.scalar.copy(out=q_bf[:], in_=q_raw[:].rearrange("p j w -> p w j"))
+        q_bf = pool.tile([P, NQ, PACK], BF16, name="q_bf", align_bytes=64)
+        nc.scalar.copy(
+            out=q_bf[:].rearrange("p (c i) j -> p c j i", i=PACK), in_=q_raw[:].rearrange("p j (c i) -> p c j i", i=PACK)
+        )
         q_codes = pool.tile([P, NQ], U32, name="q_codes", align_bytes=64)
         q_scales = pool.tile([P, NQ], U8, name="q_scales", align_bytes=64)
 
         key_words = []
         for h in range(N // GATHER):
-            tag = "q_bf_then_keys" if h == 1 else "first_keys"
+            tag = "q_raw_then_keys" if h == 1 else "first_keys"
             kw = pool.tile([P, GATHER], U32, name=f"key_words{h}", tag=tag, align_bytes=64)
             cols = slice(h * GATHER // 16, (h + 1) * GATHER // 16)
             nc.vector.tensor_copy(out=kw[:], in_=words[:].bitcast(U32).indirect(offsets[:, cols]))
@@ -69,7 +72,7 @@ def tile_attend_page_margin_kernel(tc, qT, k_words, k_scales, th, offs, out):
                 )
 
         one_less_thr = pool.tile([P, 1], F32, name="one_less_thr")
-        nc.vector.tensor_scalar(out=one_less_thr[:], in0=thr[:], scalar1=-1.0, scalar2=1.0, op0=ALU.mult, op1=ALU.add)
+        nc.scalar.activation(out=one_less_thr[:], in_=thr[:], func=ACT.Copy, scale=-1.0, bias=1.0)
 
         best = pool.tile([P, N // SEG], F32, name="best")
         for m in range(N // MM):

@@ -20,6 +20,7 @@ NQ = 128
 SEG = 32
 GATHER = 512
 MM = 256
+ROW0 = P - 16
 
 FLOPS = 2 * 512 * NQ * N
 
@@ -34,23 +35,23 @@ def tile_attend_page_margin_kernel(tc, qT, k_words, k_scales, th, offs, out):
         nc.sync.dma_start(offsets[:], offs)
 
         scales = pool.tile([P, T // 4], I32, name="scales", align_bytes=64)
-        nc.vector.memset(scales[:], 0)
+        nc.vector.memset(scales[0:ROW0, :], 0)
         key_scales = pool.tile([P, N // 4], I32, name="key_scales", align_bytes=64)
         nc.vector.memset(key_scales[:], 0)
-        nc.sync.dma_start(out=scales[4:P:8, :], in_=k_scales[0].bitcast(I32))
+        nc.sync.dma_start(out=scales[ROW0:P, :], in_=k_scales[0].bitcast(I32))
 
         words = pool.tile([P, T], I32, name="words", align_bytes=64)
         words_hbm = k_words[0].rearrange("p n t -> p (n t)").bitcast(I32)
-        nc.scalar.dma_start(out=words[:], in_=words_hbm, max_dma_last_dim=4096)
+        nc.sync.dma_start(out=words[:], in_=words_hbm, max_dma_last_dim=4096)
         q_raw = pool.tile([P, PACK, NQ], F32, name="q_raw", tag="q_raw_then_keys", align_bytes=64)
-        nc.scalar.dma_start(out=q_raw[:], in_=qT[0].rearrange("(p j) w -> p j w", j=PACK))
+        nc.sync.dma_start(out=q_raw[:], in_=qT[0].rearrange("(p j) w -> p j w", j=PACK))
         thr = pool.tile([P, 1], F32, name="thr")
-        nc.scalar.dma_start(out=thr[:], in_=th[0])
+        nc.sync.dma_start(out=thr[:], in_=th[0])
 
         picked = pool.tile([P, N], U8, name="picked", align_bytes=64)
         nc.vector.tensor_copy(out=picked[:], in_=scales[:].bitcast(U8).indirect(offsets[:]))
         for r in range(4):
-            nc.sync.dma_start(out=key_scales[r:P:32, :], in_=picked[8 * r + 4 : P : 32, :].bitcast(I32))
+            nc.sync.dma_start(out=key_scales[r:P:32, :], in_=picked[ROW0 + r : P : 4, :].bitcast(I32))
 
         q_bf = pool.tile([P, NQ, PACK], BF16, name="q_bf", align_bytes=64)
         nc.scalar.copy(

@@ -19,8 +19,11 @@ N = 1024
 NQ = 128
 SEG = 32
 GATHER = 512
-MM = 256
-ROW0 = P - 16
+PASSES = ((0, 256), (256, 256), (512, 128), (640, 128), (768, 128), (896, 128))
+ROW0 = 11
+ROW_STEP = 7
+HEADS = 1
+HEAD = 1024
 
 FLOPS = 2 * 512 * NQ * N
 
@@ -34,24 +37,29 @@ def tile_attend_page_margin_kernel(tc, qT, k_words, k_scales, th, offs, out):
         offsets = pool.tile([P, N // 16], U16, name="offsets")
         nc.sync.dma_start(offsets[:], offs)
 
-        scales = pool.tile([P, T // 4], I32, name="scales", align_bytes=64)
-        nc.vector.memset(scales[0:ROW0, :], 0)
+        scales = pool.tile([P, T // 4], I32, name="scales", tag="scales_then_thr", align_bytes=64)
+        nc.vector.memset(scales[:], 0)
         key_scales = pool.tile([P, N // 4], I32, name="key_scales", align_bytes=64)
         nc.vector.memset(key_scales[:], 0)
-        nc.sync.dma_start(out=scales[ROW0:P, :], in_=k_scales[0].bitcast(I32))
 
         words = pool.tile([P, T], I32, name="words", align_bytes=64)
         words_hbm = k_words[0].rearrange("p n t -> p (n t)").bitcast(I32)
-        nc.sync.dma_start(out=words[:], in_=words_hbm, max_dma_last_dim=4096)
+        for c in range(HEADS):
+            cols = slice(c * HEAD, (c + 1) * HEAD)
+            nc.sync.dma_start(out=words[:, cols], in_=words_hbm[:, cols])
+        nc.sync.dma_start(out=scales[ROW0 : ROW0 + 16 * ROW_STEP : ROW_STEP, :], in_=k_scales[0].bitcast(I32))
+        rest = slice(HEADS * HEAD, T)
+        nc.sync.dma_start(out=words[:, rest], in_=words_hbm[:, rest], max_dma_last_dim=4096)
         q_raw = pool.tile([P, PACK, NQ], F32, name="q_raw", tag="q_raw_then_keys", align_bytes=64)
         nc.sync.dma_start(out=q_raw[:], in_=qT[0].rearrange("(p j) w -> p j w", j=PACK))
-        thr = pool.tile([P, 1], F32, name="thr")
-        nc.sync.dma_start(out=thr[:], in_=th[0])
 
         picked = pool.tile([P, N], U8, name="picked", align_bytes=64)
         nc.vector.tensor_copy(out=picked[:], in_=scales[:].bitcast(U8).indirect(offsets[:]))
         for r in range(4):
-            nc.sync.dma_start(out=key_scales[r:P:32, :], in_=picked[ROW0 + r : P : 4, :].bitcast(I32))
+            nc.sync.dma_start(out=key_scales[r:P:32, :], in_=picked[ROW0 + ROW_STEP * r : ROW0 + 16 * ROW_STEP : 4 * ROW_STEP, :].bitcast(I32))
+
+        thr = pool.tile([P, 1], F32, name="thr", tag="scales_then_thr", align_bytes=64)
+        nc.sync.dma_start(out=thr[:], in_=th[0])
 
         q_bf = pool.tile([P, NQ, PACK], BF16, name="q_bf", align_bytes=64)
         nc.scalar.copy(
@@ -76,21 +84,21 @@ def tile_attend_page_margin_kernel(tc, qT, k_words, k_scales, th, offs, out):
         nc.scalar.activation(out=one_less_thr[:], in_=thr[:], func=ACT.Copy, scale=-1.0, bias=1.0)
 
         best = pool.tile([P, N // SEG], F32, name="best")
-        for m in range(N // MM):
-            h, c0 = divmod(m * MM, GATHER)
+        for m, (s0, width) in enumerate(PASSES):
+            h, c0 = divmod(s0, GATHER)
             scores = psum.tile([P, 512], F32, name=f"scores{m}")
             nc.tensor.matmul_mx(
-                out=scores[:, 0:MM],
+                out=scores[:, 0:width],
                 lhsT=q_codes[:].bitcast(FP8X4),
                 lhsT_scale=q_scales[:],
-                rhs=key_words[h][:, c0 : c0 + MM].bitcast(FP8X4),
-                rhs_scale=key_scales[:].bitcast(U8)[:, m * MM : (m + 1) * MM],
+                rhs=key_words[h][:, c0 : c0 + width].bitcast(FP8X4),
+                rhs_scale=key_scales[:].bitcast(U8)[:, s0 : s0 + width],
                 start=True,
                 stop=True,
             )
             nc.vector.tensor_reduce(
-                out=best[:, m * MM // SEG : (m + 1) * MM // SEG],
-                in_=scores[:, 0:MM].rearrange("p (j s) -> p j s", s=SEG),
+                out=best[:, s0 // SEG : (s0 + width) // SEG],
+                in_=scores[:, 0:width].rearrange("p (j s) -> p j s", s=SEG),
                 axis=mybir.AxisListType.X,
                 op=ALU.max,
             )
@@ -102,9 +110,10 @@ def tile_attend_page_margin_kernel(tc, qT, k_words, k_scales, th, offs, out):
         parts = (slice(0, 24), slice(24, 32))
         for c in parts:
             nc.vector.tensor_scalar(out=denom[:, c], in0=best[:, c], scalar1=one_less_thr[:], scalar2=1.0, op0=ALU.add, op1=ALU.max)
-            nc.vector.tensor_scalar(out=margin[:, c], in0=best[:, c], scalar1=thr[:], scalar2=0.0, op0=ALU.subtract, op1=ALU.max)
         for c in parts:
             nc.vector.reciprocal(out=inv[:, c], in_=denom[:, c])
+        for c in parts:
+            nc.vector.tensor_scalar(out=margin[:, c], in0=best[:, c], scalar1=thr[:], scalar2=0.0, op0=ALU.subtract, op1=ALU.max)
         for c in parts:
             nc.vector.tensor_tensor(out=res[:, c], in0=margin[:, c], in1=inv[:, c], op=ALU.mult)
         nc.sync.dma_start(out=out[0], in_=res[:])

@@ -23,7 +23,7 @@ PASSES = ((0, 256), (256, 256), (512, 128), (640, 128), (768, 128), (896, 128))
 ROW0 = 11
 ROW_STEP = 7
 HEADS = 1
-HEAD = 1024
+HEAD = 1280
 
 FLOPS = 2 * 512 * NQ * N
 
@@ -35,7 +35,6 @@ def tile_attend_page_margin_kernel(tc, qT, k_words, k_scales, th, offs, out):
         psum = ctx.enter_context(tc.psum_pool(name="psum", bufs=1))
 
         offsets = pool.tile([P, N // 16], U16, name="offsets")
-        nc.sync.dma_start(offsets[:], offs)
 
         scales = pool.tile([P, T // 4], I32, name="scales", tag="scales_then_thr", align_bytes=64)
         nc.vector.memset(scales[:], 0)
@@ -47,9 +46,10 @@ def tile_attend_page_margin_kernel(tc, qT, k_words, k_scales, th, offs, out):
         for c in range(HEADS):
             cols = slice(c * HEAD, (c + 1) * HEAD)
             nc.sync.dma_start(out=words[:, cols], in_=words_hbm[:, cols])
+        nc.sync.dma_start(offsets[:], offs)
         nc.sync.dma_start(out=scales[ROW0 : ROW0 + 16 * ROW_STEP : ROW_STEP, :], in_=k_scales[0].bitcast(I32))
         rest = slice(HEADS * HEAD, T)
-        nc.sync.dma_start(out=words[:, rest], in_=words_hbm[:, rest], max_dma_last_dim=4096)
+        nc.sync.dma_start(out=words[:, rest], in_=words_hbm[:, rest])
         q_raw = pool.tile([P, PACK, NQ], F32, name="q_raw", tag="q_raw_then_keys", align_bytes=64)
         nc.sync.dma_start(out=q_raw[:], in_=qT[0].rearrange("(p j) w -> p j w", j=PACK))
 
@@ -107,7 +107,7 @@ def tile_attend_page_margin_kernel(tc, qT, k_words, k_scales, th, offs, out):
         margin = pool.tile([P, N // SEG], F32, name="margin")
         inv = pool.tile([P, N // SEG], F32, name="inv")
         res = pool.tile([P, N // SEG], F32, name="res")
-        parts = (slice(0, 24), slice(24, 32))
+        parts = (slice(0, 16), slice(16, 28), slice(28, 32))
         for c in parts:
             nc.vector.tensor_scalar(out=denom[:, c], in0=best[:, c], scalar1=one_less_thr[:], scalar2=1.0, op0=ALU.add, op1=ALU.max)
         for c in parts:

@@ -22,8 +22,7 @@ GATHER = 512
 PASSES = ((0, 256), (256, 256), (512, 128), (640, 128), (768, 128), (896, 128))
 ROW0 = 11
 ROW_STEP = 7
-HEADS = 1
-HEAD = 1280
+HEAD = 384
 
 FLOPS = 2 * 512 * NQ * N
 
@@ -37,21 +36,19 @@ def tile_attend_page_margin_kernel(tc, qT, k_words, k_scales, th, offs, out):
         offsets = pool.tile([P, N // 16], U16, name="offsets")
 
         scales = pool.tile([P, T // 4], I32, name="scales", tag="scales_then_thr", align_bytes=64)
-        nc.vector.memset(scales[:], 0)
+        nc.vector.memset(scales[:, : T // 8], 0)
+        nc.gpsimd.memset(scales[:, T // 8 :], 0)
         key_scales = pool.tile([P, N // 4], I32, name="key_scales", align_bytes=64)
         nc.vector.memset(key_scales[:], 0)
 
         words = pool.tile([P, T], I32, name="words", align_bytes=64)
         words_hbm = k_words[0].rearrange("p n t -> p (n t)").bitcast(I32)
-        for c in range(HEADS):
-            cols = slice(c * HEAD, (c + 1) * HEAD)
-            nc.sync.dma_start(out=words[:, cols], in_=words_hbm[:, cols])
+        q_raw = pool.tile([P, PACK, NQ], F32, name="q_raw", align_bytes=64)
+        nc.sync.dma_start(out=q_raw[:], in_=qT[0].rearrange("(p j) w -> p j w", j=PACK))
+        nc.sync.dma_start(out=words[:, :HEAD], in_=words_hbm[:, :HEAD])
         nc.sync.dma_start(offsets[:], offs)
         nc.sync.dma_start(out=scales[ROW0 : ROW0 + 16 * ROW_STEP : ROW_STEP, :], in_=k_scales[0].bitcast(I32))
-        rest = slice(HEADS * HEAD, T)
-        nc.sync.dma_start(out=words[:, rest], in_=words_hbm[:, rest])
-        q_raw = pool.tile([P, PACK, NQ], F32, name="q_raw", tag="q_raw_then_keys", align_bytes=64)
-        nc.sync.dma_start(out=q_raw[:], in_=qT[0].rearrange("(p j) w -> p j w", j=PACK))
+        nc.sync.dma_start(out=words[:, HEAD:], in_=words_hbm[:, HEAD:])
 
         picked = pool.tile([P, N], U8, name="picked", align_bytes=64)
         nc.vector.tensor_copy(out=picked[:], in_=scales[:].bitcast(U8).indirect(offsets[:]))
@@ -67,18 +64,14 @@ def tile_attend_page_margin_kernel(tc, qT, k_words, k_scales, th, offs, out):
         )
         q_codes = pool.tile([P, NQ], U32, name="q_codes", align_bytes=64)
         q_scales = pool.tile([P, NQ], U8, name="q_scales", align_bytes=64)
+        nc.vector.quantize_mx(out=q_codes[:].bitcast(FP8X4), scales=q_scales[:], in_=q_bf[:].rearrange("p w j -> p (w j)"))
 
         key_words = []
         for h in range(N // GATHER):
-            tag = "q_raw_then_keys" if h == 1 else "first_keys"
-            kw = pool.tile([P, GATHER], U32, name=f"key_words{h}", tag=tag, align_bytes=64)
+            kw = pool.tile([P, GATHER], U32, name=f"key_words{h}", align_bytes=64)
             cols = slice(h * GATHER // 16, (h + 1) * GATHER // 16)
             nc.vector.tensor_copy(out=kw[:], in_=words[:].bitcast(U32).indirect(offsets[:, cols]))
             key_words.append(kw)
-            if h == 0:
-                nc.vector.quantize_mx(
-                    out=q_codes[:].bitcast(FP8X4), scales=q_scales[:], in_=q_bf[:].rearrange("p w j -> p (w j)")
-                )
 
         one_less_thr = pool.tile([P, 1], F32, name="one_less_thr")
         nc.scalar.activation(out=one_less_thr[:], in_=thr[:], func=ACT.Copy, scale=-1.0, bias=1.0)

@@ -50,18 +50,19 @@ def tile_attend_page_margin_kernel(tc, qT, k_words, k_scales, th, offs, out):
         nc.sync.dma_start(out=scales[ROW0 : ROW0 + 16 * ROW_STEP : ROW_STEP, :], in_=k_scales[0].bitcast(I32))
         nc.sync.dma_start(out=words[:, HEAD:], in_=words_hbm[:, HEAD:])
 
-        picked = pool.tile([P, N], U8, name="picked", align_bytes=64)
-        nc.vector.tensor_copy(out=picked[:], in_=scales[:].bitcast(U8).indirect(offsets[:]))
-        for r in range(4):
-            nc.sync.dma_start(out=key_scales[r:P:32, :], in_=picked[ROW0 + ROW_STEP * r : ROW0 + 16 * ROW_STEP : 4 * ROW_STEP, :].bitcast(I32))
-
-        thr = pool.tile([P, 1], F32, name="thr", tag="scales_then_thr", align_bytes=64)
-        nc.sync.dma_start(out=thr[:], in_=th[0])
-
         q_bf = pool.tile([P, NQ, PACK], BF16, name="q_bf", align_bytes=64)
         nc.scalar.copy(
             out=q_bf[:].rearrange("p (c i) j -> p c j i", i=PACK), in_=q_raw[:].rearrange("p j (c i) -> p c j i", i=PACK)
         )
+
+        picked = pool.tile([P, N], U8, name="picked", align_bytes=64)
+        nc.vector.tensor_copy(out=picked[:], in_=scales[:].bitcast(U8).indirect(offsets[:]))
+        for r in range(4):
+            nc.scalar.dma_start(out=key_scales[r:P:32, :], in_=picked[ROW0 + ROW_STEP * r : ROW0 + 16 * ROW_STEP : 4 * ROW_STEP, :].bitcast(I32))
+
+        thr = pool.tile([P, 1], F32, name="thr", tag="scales_then_thr", align_bytes=64)
+        nc.sync.dma_start(out=thr[:], in_=th[0])
+
         q_codes = pool.tile([P, NQ], U32, name="q_codes", align_bytes=64)
         q_scales = pool.tile([P, NQ], U8, name="q_scales", align_bytes=64)
         nc.vector.quantize_mx(out=q_codes[:].bitcast(FP8X4), scales=q_scales[:], in_=q_bf[:].rearrange("p w j -> p (w j)"))

@@ -10,7 +10,6 @@ U16 = mybir.dt.uint16
 U8 = mybir.dt.uint8
 FP8X4 = mybir.dt.float8_e4m3fn_x4
 ALU = mybir.AluOpType
-ACT = mybir.ActivationFunctionType
 
 P = 128
 PACK = 4
@@ -35,7 +34,7 @@ def tile_attend_page_margin_kernel(tc, qT, k_words, k_scales, th, offs, out):
 
         offsets = pool.tile([P, N // 16], U16, name="offsets")
 
-        scales = pool.tile([P, T // 4], I32, name="scales", tag="scales_then_thr", align_bytes=64)
+        scales = pool.tile([P, T // 4], I32, name="scales", align_bytes=64)
         nc.vector.memset(scales[:, : T // 8], 0)
         nc.gpsimd.memset(scales[:, T // 8 :], 0)
         key_scales = pool.tile([P, N // 4], I32, name="key_scales", align_bytes=64)
@@ -50,8 +49,11 @@ def tile_attend_page_margin_kernel(tc, qT, k_words, k_scales, th, offs, out):
         nc.sync.dma_start(out=scales[ROW0 : ROW0 + 16 * ROW_STEP : ROW_STEP, :], in_=k_scales[0].bitcast(I32))
         nc.sync.dma_start(out=words[:, HEAD:], in_=words_hbm[:, HEAD:])
 
+        thr = pool.tile([P, 1], F32, name="thr")
+        nc.sync.dma_start(out=thr[:], in_=th[0])
+
         q_bf = pool.tile([P, NQ, PACK], BF16, name="q_bf", align_bytes=64)
-        nc.scalar.copy(
+        nc.vector.tensor_copy(
             out=q_bf[:].rearrange("p (c i) j -> p c j i", i=PACK), in_=q_raw[:].rearrange("p j (c i) -> p c j i", i=PACK)
         )
 
@@ -60,8 +62,6 @@ def tile_attend_page_margin_kernel(tc, qT, k_words, k_scales, th, offs, out):
         for r in range(4):
             nc.scalar.dma_start(out=key_scales[r:P:32, :], in_=picked[ROW0 + ROW_STEP * r : ROW0 + 16 * ROW_STEP : 4 * ROW_STEP, :].bitcast(I32))
 
-        thr = pool.tile([P, 1], F32, name="thr", tag="scales_then_thr", align_bytes=64)
-        nc.sync.dma_start(out=thr[:], in_=th[0])
 
         q_codes = pool.tile([P, NQ], U32, name="q_codes", align_bytes=64)
         q_scales = pool.tile([P, NQ], U8, name="q_scales", align_bytes=64)
@@ -75,7 +75,7 @@ def tile_attend_page_margin_kernel(tc, qT, k_words, k_scales, th, offs, out):
             key_words.append(kw)
 
         one_less_thr = pool.tile([P, 1], F32, name="one_less_thr")
-        nc.scalar.activation(out=one_less_thr[:], in_=thr[:], func=ACT.Copy, scale=-1.0, bias=1.0)
+        nc.vector.tensor_scalar(out=one_less_thr[:], in0=thr[:], scalar1=-1.0, scalar2=1.0, op0=ALU.mult, op1=ALU.add)
 
         best = pool.tile([P, N // SEG], F32, name="best")
         for m, (s0, width) in enumerate(PASSES):

@@ -21,7 +21,7 @@ GATHER = 512
 PASSES = ((0, 256), (256, 256), (512, 128), (640, 128), (768, 128), (896, 128))
 ROW0 = 11
 ROW_STEP = 7
-HEAD = 384
+HEAD = 640
 
 FLOPS = 2 * 512 * NQ * N
 
@@ -35,18 +35,17 @@ def tile_attend_page_margin_kernel(tc, qT, k_words, k_scales, th, offs, out):
         offsets = pool.tile([P, N // 16], U16, name="offsets")
 
         scales = pool.tile([P, T // 4], I32, name="scales", align_bytes=64)
-        nc.vector.memset(scales[:, : T // 8], 0)
-        nc.gpsimd.memset(scales[:, T // 8 :], 0)
+        nc.vector.memset(scales[:], 0)
         key_scales = pool.tile([P, N // 4], I32, name="key_scales", align_bytes=64)
         nc.vector.memset(key_scales[:], 0)
 
         words = pool.tile([P, T], I32, name="words", align_bytes=64)
         words_hbm = k_words[0].rearrange("p n t -> p (n t)").bitcast(I32)
-        q_raw = pool.tile([P, PACK, NQ], F32, name="q_raw", align_bytes=64)
-        nc.sync.dma_start(out=q_raw[:], in_=qT[0].rearrange("(p j) w -> p j w", j=PACK))
         nc.sync.dma_start(out=words[:, :HEAD], in_=words_hbm[:, :HEAD])
         nc.sync.dma_start(offsets[:], offs)
         nc.sync.dma_start(out=scales[ROW0 : ROW0 + 16 * ROW_STEP : ROW_STEP, :], in_=k_scales[0].bitcast(I32))
+        q_raw = pool.tile([P, PACK, NQ], F32, name="q_raw", align_bytes=64)
+        nc.sync.dma_start(out=q_raw[:], in_=qT[0].rearrange("(p j) w -> p j w", j=PACK))
         nc.sync.dma_start(out=words[:, HEAD:], in_=words_hbm[:, HEAD:])
 
         thr = pool.tile([P, 1], F32, name="thr")

@@ -21,7 +21,6 @@ GATHER = 512
 PASSES = ((0, 256), (256, 256), (512, 128), (640, 128), (768, 128), (896, 128))
 ROW0 = 11
 ROW_STEP = 7
-HEAD = 640
 
 FLOPS = 2 * 512 * NQ * N
 
@@ -41,15 +40,15 @@ def tile_attend_page_margin_kernel(tc, qT, k_words, k_scales, th, offs, out):
 
         words = pool.tile([P, T], I32, name="words", align_bytes=64)
         words_hbm = k_words[0].rearrange("p n t -> p (n t)").bitcast(I32)
-        nc.sync.dma_start(out=words[:, :HEAD], in_=words_hbm[:, :HEAD])
-        nc.sync.dma_start(offsets[:], offs)
-        nc.sync.dma_start(out=scales[ROW0 : ROW0 + 16 * ROW_STEP : ROW_STEP, :], in_=k_scales[0].bitcast(I32))
         q_raw = pool.tile([P, PACK, NQ], F32, name="q_raw", align_bytes=64)
         nc.sync.dma_start(out=q_raw[:], in_=qT[0].rearrange("(p j) w -> p j w", j=PACK))
-        nc.sync.dma_start(out=words[:, HEAD:], in_=words_hbm[:, HEAD:])
-
-        thr = pool.tile([P, 1], F32, name="thr")
-        nc.sync.dma_start(out=thr[:], in_=th[0])
+        nc.sync.dma_start(offsets[:], offs)
+        th_rows = pool.tile([P, 32], F32, name="th_rows", align_bytes=64)
+        nc.sync.dma_start(out=th_rows[31:P:32, :], in_=th[0].rearrange("(g i) o -> g (i o)", i=32))
+        nc.sync.dma_start(out=scales[ROW0 : ROW0 + 16 * ROW_STEP : ROW_STEP, :], in_=k_scales[0].bitcast(I32))
+        nc.sync.dma_start(out=words[:], in_=words_hbm)
+        for g in range(4):
+            nc.vector.memset(th_rows[32 * g : 32 * g + 31, :], 0.0)
 
         q_bf = pool.tile([P, NQ, PACK], BF16, name="q_bf", align_bytes=64)
         nc.vector.tensor_copy(
@@ -66,15 +65,18 @@ def tile_attend_page_margin_kernel(tc, qT, k_words, k_scales, th, offs, out):
         q_scales = pool.tile([P, NQ], U8, name="q_scales", align_bytes=64)
         nc.vector.quantize_mx(out=q_codes[:].bitcast(FP8X4), scales=q_scales[:], in_=q_bf[:].rearrange("p w j -> p (w j)"))
 
+        th_cols = pool.tile([P, 32], F32, name="th_cols", align_bytes=64)
+        nc.vector.transpose(out=th_cols[:], in_=th_rows[:])
+        thr = th_cols[:, 31:32]
+        one_less_thr = pool.tile([P, 1], F32, name="one_less_thr")
+        nc.vector.tensor_scalar(out=one_less_thr[:], in0=thr, scalar1=-1.0, scalar2=1.0, op0=ALU.mult, op1=ALU.add)
+
         key_words = []
         for h in range(N // GATHER):
             kw = pool.tile([P, GATHER], U32, name=f"key_words{h}", align_bytes=64)
             cols = slice(h * GATHER // 16, (h + 1) * GATHER // 16)
             nc.vector.tensor_copy(out=kw[:], in_=words[:].bitcast(U32).indirect(offsets[:, cols]))
             key_words.append(kw)
-
-        one_less_thr = pool.tile([P, 1], F32, name="one_less_thr")
-        nc.vector.tensor_scalar(out=one_less_thr[:], in0=thr[:], scalar1=-1.0, scalar2=1.0, op0=ALU.mult, op1=ALU.add)
 
         best = pool.tile([P, N // SEG], F32, name="best")
         for m, (s0, width) in enumerate(PASSES):
@@ -106,7 +108,7 @@ def tile_attend_page_margin_kernel(tc, qT, k_words, k_scales, th, offs, out):
         for c in parts:
             nc.vector.reciprocal(out=inv[:, c], in_=denom[:, c])
         for c in parts:
-            nc.vector.tensor_scalar(out=margin[:, c], in0=best[:, c], scalar1=thr[:], scalar2=0.0, op0=ALU.subtract, op1=ALU.max)
+            nc.vector.tensor_scalar(out=margin[:, c], in0=best[:, c], scalar1=thr, scalar2=0.0, op0=ALU.subtract, op1=ALU.max)
         for c in parts:
             nc.vector.tensor_tensor(out=res[:, c], in0=margin[:, c], in1=inv[:, c], op=ALU.mult)
         nc.sync.dma_start(out=out[0], in_=res[:])

@@ -17,12 +17,19 @@ T = 4096
 N = 1024
 NQ = 128
 SEG = 32
-GATHER = 512
-PASSES = ((0, 256), (256, 256), (512, 128), (640, 128), (768, 128), (896, 128))
+PAGES = N // SEG
+GATHERS = (256, 256, 256, 256,)
+PASSES = (128, 128, 256, 256, 128, 128,)
+PARTS = (16, 12, 4,)
 ROW0 = 11
 ROW_STEP = 7
 
 FLOPS = 2 * 512 * NQ * N
+
+
+def runs(widths):
+    starts = [sum(widths[:i]) for i in range(len(widths))]
+    return list(zip(starts, widths))
 
 
 def tile_attend_page_margin_kernel(tc, qT, k_words, k_scales, th, offs, out):
@@ -32,21 +39,20 @@ def tile_attend_page_margin_kernel(tc, qT, k_words, k_scales, th, offs, out):
         psum = ctx.enter_context(tc.psum_pool(name="psum", bufs=1))
 
         offsets = pool.tile([P, N // 16], U16, name="offsets")
-
         scales = pool.tile([P, T // 4], I32, name="scales", align_bytes=64)
-        nc.vector.memset(scales[:], 0)
         key_scales = pool.tile([P, N // 4], I32, name="key_scales", align_bytes=64)
+        words = pool.tile([P, T], I32, name="words", align_bytes=64)
+        q_raw = pool.tile([P, PACK, NQ], F32, name="q_raw", align_bytes=64)
+        th_rows = pool.tile([P, 32], F32, name="th_rows", align_bytes=64)
+
+        nc.vector.memset(scales[:], 0)
         nc.vector.memset(key_scales[:], 0)
 
-        words = pool.tile([P, T], I32, name="words", align_bytes=64)
-        words_hbm = k_words[0].rearrange("p n t -> p (n t)").bitcast(I32)
-        q_raw = pool.tile([P, PACK, NQ], F32, name="q_raw", align_bytes=64)
         nc.sync.dma_start(out=q_raw[:], in_=qT[0].rearrange("(p j) w -> p j w", j=PACK))
         nc.sync.dma_start(offsets[:], offs)
-        th_rows = pool.tile([P, 32], F32, name="th_rows", align_bytes=64)
         nc.sync.dma_start(out=th_rows[31:P:32, :], in_=th[0].rearrange("(g i) o -> g (i o)", i=32))
         nc.sync.dma_start(out=scales[ROW0 : ROW0 + 16 * ROW_STEP : ROW_STEP, :], in_=k_scales[0].bitcast(I32))
-        nc.sync.dma_start(out=words[:], in_=words_hbm)
+        nc.sync.dma_start(out=words[:], in_=k_words[0].rearrange("p n t -> p (n t)").bitcast(I32))
         for g in range(4):
             nc.vector.memset(th_rows[32 * g : 32 * g + 31, :], 0.0)
 
@@ -60,33 +66,30 @@ def tile_attend_page_margin_kernel(tc, qT, k_words, k_scales, th, offs, out):
         for r in range(4):
             nc.scalar.dma_start(out=key_scales[r:P:32, :], in_=picked[ROW0 + ROW_STEP * r : ROW0 + 16 * ROW_STEP : 4 * ROW_STEP, :].bitcast(I32))
 
-
         q_codes = pool.tile([P, NQ], U32, name="q_codes", align_bytes=64)
         q_scales = pool.tile([P, NQ], U8, name="q_scales", align_bytes=64)
         nc.vector.quantize_mx(out=q_codes[:].bitcast(FP8X4), scales=q_scales[:], in_=q_bf[:].rearrange("p w j -> p (w j)"))
 
         th_cols = pool.tile([P, 32], F32, name="th_cols", align_bytes=64)
         nc.vector.transpose(out=th_cols[:], in_=th_rows[:])
-        thr = th_cols[:, 31:32]
         one_less_thr = pool.tile([P, 1], F32, name="one_less_thr")
-        nc.vector.tensor_scalar(out=one_less_thr[:], in0=thr, scalar1=-1.0, scalar2=1.0, op0=ALU.mult, op1=ALU.add)
+        nc.vector.tensor_scalar(out=one_less_thr[:], in0=th_cols[:, 31:32], scalar1=-1.0, scalar2=1.0, op0=ALU.mult, op1=ALU.add)
 
-        key_words = []
-        for h in range(N // GATHER):
-            kw = pool.tile([P, GATHER], U32, name=f"key_words{h}", align_bytes=64)
-            cols = slice(h * GATHER // 16, (h + 1) * GATHER // 16)
-            nc.vector.tensor_copy(out=kw[:], in_=words[:].bitcast(U32).indirect(offsets[:, cols]))
-            key_words.append(kw)
+        gathered = []
+        for h, (s0, width) in enumerate(runs(GATHERS)):
+            kw = pool.tile([P, width], U32, name=f"key_words{h}", align_bytes=64)
+            nc.vector.tensor_copy(out=kw[:], in_=words[:].bitcast(U32).indirect(offsets[:, s0 // 16 : (s0 + width) // 16]))
+            gathered.append((s0, width, kw))
 
-        best = pool.tile([P, N // SEG], F32, name="best")
-        for m, (s0, width) in enumerate(PASSES):
-            h, c0 = divmod(s0, GATHER)
+        best = pool.tile([P, PAGES], F32, name="best")
+        for m, (s0, width) in enumerate(runs(PASSES)):
+            g0, kw = [(g0, kw) for g0, gw, kw in gathered if g0 <= s0 < g0 + gw][0]
             scores = psum.tile([P, 512], F32, name=f"scores{m}")
             nc.tensor.matmul_mx(
                 out=scores[:, 0:width],
                 lhsT=q_codes[:].bitcast(FP8X4),
                 lhsT_scale=q_scales[:],
-                rhs=key_words[h][:, c0 : c0 + width].bitcast(FP8X4),
+                rhs=kw[:, s0 - g0 : s0 - g0 + width].bitcast(FP8X4),
                 rhs_scale=key_scales[:].bitcast(U8)[:, s0 : s0 + width],
                 start=True,
                 stop=True,
@@ -98,17 +101,14 @@ def tile_attend_page_margin_kernel(tc, qT, k_words, k_scales, th, offs, out):
                 op=ALU.max,
             )
 
-        denom = pool.tile([P, N // SEG], F32, name="denom")
-        margin = pool.tile([P, N // SEG], F32, name="margin")
-        inv = pool.tile([P, N // SEG], F32, name="inv")
-        res = pool.tile([P, N // SEG], F32, name="res")
-        parts = (slice(0, 16), slice(16, 28), slice(28, 32))
+        denom = pool.tile([P, PAGES], F32, name="denom")
+        inv = pool.tile([P, PAGES], F32, name="inv")
+        res = pool.tile([P, PAGES], F32, name="res")
+        parts = [slice(j0, j0 + n) for j0, n in runs(PARTS)]
         for c in parts:
             nc.vector.tensor_scalar(out=denom[:, c], in0=best[:, c], scalar1=one_less_thr[:], scalar2=1.0, op0=ALU.add, op1=ALU.max)
         for c in parts:
             nc.vector.reciprocal(out=inv[:, c], in_=denom[:, c])
         for c in parts:
-            nc.vector.tensor_scalar(out=margin[:, c], in0=best[:, c], scalar1=thr, scalar2=0.0, op0=ALU.subtract, op1=ALU.max)
-        for c in parts:
-            nc.vector.tensor_tensor(out=res[:, c], in0=margin[:, c], in1=inv[:, c], op=ALU.mult)
+            nc.vector.tensor_scalar(out=res[:, c], in0=inv[:, c], scalar1=-1.0, scalar2=1.0, op0=ALU.mult, op1=ALU.add)
         nc.sync.dma_start(out=out[0], in_=res[:])

@@ -39,7 +39,7 @@ def tile_attend_page_margin_kernel(tc, qT, k_words, k_scales, th, offs, out):
         psum = ctx.enter_context(tc.psum_pool(name="psum", bufs=1))
 
         offsets = pool.tile([P, N // 16], U16, name="offsets")
-        scales = pool.tile([P, T // 4], I32, name="scales", align_bytes=64)
+        scales = pool.tile([P, T // 4], I32, name="scales", tag="window_then_codes", align_bytes=64)
         key_scales = pool.tile([P, N // 4], I32, name="key_scales", align_bytes=64)
         words = pool.tile([P, T], I32, name="words", align_bytes=64)
         q_raw = pool.tile([P, PACK, NQ], F32, name="q_raw", align_bytes=64)
@@ -64,9 +64,10 @@ def tile_attend_page_margin_kernel(tc, qT, k_words, k_scales, th, offs, out):
         picked = pool.tile([P, N], U8, name="picked", align_bytes=64)
         nc.vector.tensor_copy(out=picked[:], in_=scales[:].bitcast(U8).indirect(offsets[:]))
         for r in range(4):
-            nc.scalar.dma_start(out=key_scales[r:P:32, :], in_=picked[ROW0 + ROW_STEP * r : ROW0 + 16 * ROW_STEP : 4 * ROW_STEP, :].bitcast(I32))
+            queue = nc.scalar if r % 2 == 0 else nc.sync
+            queue.dma_start(out=key_scales[r:P:32, :], in_=picked[ROW0 + ROW_STEP * r : ROW0 + 16 * ROW_STEP : 4 * ROW_STEP, :].bitcast(I32))
 
-        q_codes = pool.tile([P, NQ], U32, name="q_codes", align_bytes=64)
+        q_codes = pool.tile([P, NQ], U32, name="q_codes", tag="window_then_codes", align_bytes=64)
         q_scales = pool.tile([P, NQ], U8, name="q_scales", align_bytes=64)
         nc.vector.quantize_mx(out=q_codes[:].bitcast(FP8X4), scales=q_scales[:], in_=q_bf[:].rearrange("p w j -> p (w j)"))
 

@@ -64,8 +64,7 @@ def tile_attend_page_margin_kernel(tc, qT, k_words, k_scales, th, offs, out):
         picked = pool.tile([P, N], U8, name="picked", align_bytes=64)
         nc.vector.tensor_copy(out=picked[:], in_=scales[:].bitcast(U8).indirect(offsets[:]))
         for r in range(4):
-            queue = nc.scalar if r % 2 == 0 else nc.sync
-            queue.dma_start(out=key_scales[r:P:32, :], in_=picked[ROW0 + ROW_STEP * r : ROW0 + 16 * ROW_STEP : 4 * ROW_STEP, :].bitcast(I32))
+            nc.sync.dma_start(out=key_scales[r:P:32, :], in_=picked[ROW0 + ROW_STEP * r : ROW0 + 16 * ROW_STEP : 4 * ROW_STEP, :].bitcast(I32))
 
         q_codes = pool.tile([P, NQ], U32, name="q_codes", tag="window_then_codes", align_bytes=64)
         q_scales = pool.tile([P, NQ], U8, name="q_scales", align_bytes=64)

@@ -18,8 +18,8 @@ N = 1024
 NQ = 128
 SEG = 32
 PAGES = N // SEG
-GATHERS = (256, 256, 256, 256,)
-PASSES = (128, 128, 256, 256, 128, 128,)
+GATHERS = (384, 384, 256,)
+PASSES = (128, 256, 128, 256, 128, 128,)
 PARTS = (16, 12, 4,)
 ROW0 = 11
 ROW_STEP = 7

@@ -20,7 +20,7 @@ SEG = 32
 PAGES = N // SEG
 GATHERS = (384, 384, 256,)
 PASSES = (128, 256, 128, 256, 128, 128,)
-PARTS = (16, 12, 4,)
+PARTS = (24, 4, 4,)
 ROW0 = 11
 ROW_STEP = 7
 
@@ -36,10 +36,11 @@ def tile_attend_page_margin_kernel(tc, qT, k_words, k_scales, th, offs, out):
     nc = tc.nc
     with ExitStack() as ctx:
         pool = ctx.enter_context(tc.tile_pool(name="held", bufs=1))
+        shared = ctx.enter_context(tc.tile_pool(name="shared", bufs=1))
         psum = ctx.enter_context(tc.psum_pool(name="psum", bufs=1))
 
         offsets = pool.tile([P, N // 16], U16, name="offsets")
-        scales = pool.tile([P, T // 4], I32, name="scales", tag="window_then_codes", align_bytes=64)
+        scales = shared.tile([P, T // 4], I32, name="scales", align_bytes=64, offset=0)
         key_scales = pool.tile([P, N // 4], I32, name="key_scales", align_bytes=64)
         words = pool.tile([P, T], I32, name="words", align_bytes=64)
         q_raw = pool.tile([P, PACK, NQ], F32, name="q_raw", align_bytes=64)
@@ -63,15 +64,19 @@ def tile_attend_page_margin_kernel(tc, qT, k_words, k_scales, th, offs, out):
 
         picked = pool.tile([P, N], U8, name="picked", align_bytes=64)
         nc.vector.tensor_copy(out=picked[:], in_=scales[:].bitcast(U8).indirect(offsets[:]))
-        for r in range(4):
-            nc.sync.dma_start(out=key_scales[r:P:32, :], in_=picked[ROW0 + ROW_STEP * r : ROW0 + 16 * ROW_STEP : 4 * ROW_STEP, :].bitcast(I32))
+        first, second, whole = slice(0, N // 2), slice(N // 2, N), slice(0, N)
+        moves = [(r, first) for r in range(3)] + [(3, whole)] + [(r, second) for r in range(3)]
+        for r, slots in moves:
+            rows = picked[ROW0 + ROW_STEP * r : ROW0 + 16 * ROW_STEP : 4 * ROW_STEP, slots]
+            nc.sync.dma_start(out=key_scales[r:P:32, slots.start // 4 : slots.stop // 4], in_=rows.bitcast(I32))
 
-        q_codes = pool.tile([P, NQ], U32, name="q_codes", tag="window_then_codes", align_bytes=64)
+        th_cols = shared.tile([P, 32], F32, name="th_cols", align_bytes=64, offset=4 * NQ)
+        nc.vector.transpose(out=th_cols[:], in_=th_rows[:])
+
+        q_codes = shared.tile([P, NQ], U32, name="q_codes", align_bytes=64, offset=0)
         q_scales = pool.tile([P, NQ], U8, name="q_scales", align_bytes=64)
         nc.vector.quantize_mx(out=q_codes[:].bitcast(FP8X4), scales=q_scales[:], in_=q_bf[:].rearrange("p w j -> p (w j)"))
 
-        th_cols = pool.tile([P, 32], F32, name="th_cols", align_bytes=64)
-        nc.vector.transpose(out=th_cols[:], in_=th_rows[:])
         one_less_thr = pool.tile([P, 1], F32, name="one_less_thr")
         nc.vector.tensor_scalar(out=one_less_thr[:], in0=th_cols[:, 31:32], scalar1=-1.0, scalar2=1.0, op0=ALU.mult, op1=ALU.add)
 

@@ -36,11 +36,10 @@ def tile_attend_page_margin_kernel(tc, qT, k_words, k_scales, th, offs, out):
     nc = tc.nc
     with ExitStack() as ctx:
         pool = ctx.enter_context(tc.tile_pool(name="held", bufs=1))
-        shared = ctx.enter_context(tc.tile_pool(name="shared", bufs=1))
         psum = ctx.enter_context(tc.psum_pool(name="psum", bufs=1))
 
         offsets = pool.tile([P, N // 16], U16, name="offsets")
-        scales = shared.tile([P, T // 4], I32, name="scales", align_bytes=64, offset=0)
+        scales = pool.tile([P, T // 4], I32, name="scales", align_bytes=64)
         key_scales = pool.tile([P, N // 4], I32, name="key_scales", align_bytes=64)
         words = pool.tile([P, T], I32, name="words", align_bytes=64)
         q_raw = pool.tile([P, PACK, NQ], F32, name="q_raw", align_bytes=64)
@@ -68,15 +67,14 @@ def tile_attend_page_margin_kernel(tc, qT, k_words, k_scales, th, offs, out):
         moves = [(r, first) for r in range(3)] + [(3, whole)] + [(r, second) for r in range(3)]
         for r, slots in moves:
             rows = picked[ROW0 + ROW_STEP * r : ROW0 + 16 * ROW_STEP : 4 * ROW_STEP, slots]
-            nc.sync.dma_start(out=key_scales[r:P:32, slots.start // 4 : slots.stop // 4], in_=rows.bitcast(I32))
+            nc.scalar.dma_start(out=key_scales[r:P:32, slots.start // 4 : slots.stop // 4], in_=rows.bitcast(I32))
 
-        th_cols = shared.tile([P, 32], F32, name="th_cols", align_bytes=64, offset=4 * NQ)
-        nc.vector.transpose(out=th_cols[:], in_=th_rows[:])
-
-        q_codes = shared.tile([P, NQ], U32, name="q_codes", align_bytes=64, offset=0)
+        q_codes = pool.tile([P, NQ], U32, name="q_codes", align_bytes=64)
         q_scales = pool.tile([P, NQ], U8, name="q_scales", align_bytes=64)
         nc.vector.quantize_mx(out=q_codes[:].bitcast(FP8X4), scales=q_scales[:], in_=q_bf[:].rearrange("p w j -> p (w j)"))
 
+        th_cols = pool.tile([P, 32], F32, name="th_cols", align_bytes=64)
+        nc.vector.transpose(out=th_cols[:], in_=th_rows[:])
         one_less_thr = pool.tile([P, 1], F32, name="one_less_thr")
         nc.vector.tensor_scalar(out=one_less_thr[:], in0=th_cols[:, 31:32], scalar1=-1.0, scalar2=1.0, op0=ALU.mult, op1=ALU.add)
 

@@ -19,7 +19,7 @@ NQ = 128
 SEG = 32
 PAGES = N // SEG
 GATHERS = (384, 384, 256,)
-PASSES = (128, 256, 128, 256, 128, 128,)
+PASSES = (128, 128, 128, 128, 128, 128, 128, 128,)
 PARTS = (24, 4, 4,)
 ROW0 = 11
 ROW_STEP = 7
@@ -63,7 +63,7 @@ def tile_attend_page_margin_kernel(tc, qT, k_words, k_scales, th, offs, out):
 
         picked = pool.tile([P, N], U8, name="picked", align_bytes=64)
         nc.vector.tensor_copy(out=picked[:], in_=scales[:].bitcast(U8).indirect(offsets[:]))
-        first, second, whole = slice(0, N // 2), slice(N // 2, N), slice(0, N)
+        first, second, whole = slice(0, GATHERS[0]), slice(GATHERS[0], N), slice(0, N)
         moves = [(r, first) for r in range(3)] + [(3, whole)] + [(r, second) for r in range(3)]
         for r, slots in moves:
             rows = picked[ROW0 + ROW_STEP * r : ROW0 + 16 * ROW_STEP : 4 * ROW_STEP, slots]

@@ -106,12 +106,14 @@ def tile_attend_page_margin_kernel(tc, qT, k_words, k_scales, th, offs, out):
 
         denom = pool.tile([P, PAGES], F32, name="denom")
         inv = pool.tile([P, PAGES], F32, name="inv")
+        margin = pool.tile([P, PAGES], F32, name="margin")
         res = pool.tile([P, PAGES], F32, name="res")
         parts = [slice(j0, j0 + n) for j0, n in runs(PARTS)]
         for c in parts:
             nc.vector.tensor_scalar(out=denom[:, c], in0=best[:, c], scalar1=one_less_thr[:], scalar2=1.0, op0=ALU.add, op1=ALU.max)
         for c in parts:
             nc.vector.reciprocal(out=inv[:, c], in_=denom[:, c])
+        nc.vector.tensor_scalar(out=margin[:], in0=best[:], scalar1=th_cols[:, 31:32], scalar2=0.0, op0=ALU.subtract, op1=ALU.max)
         for c in parts:
-            nc.vector.tensor_scalar(out=res[:, c], in0=inv[:, c], scalar1=-1.0, scalar2=1.0, op0=ALU.mult, op1=ALU.add)
+            nc.vector.tensor_tensor(out=res[:, c], in0=margin[:, c], in1=inv[:, c], op=ALU.mult)
         nc.sync.dma_start(out=out[0], in_=res[:])

@@ -63,8 +63,9 @@ def tile_attend_page_margin_kernel(tc, qT, k_words, k_scales, th, offs, out):
 
         picked = pool.tile([P, N], U8, name="picked", align_bytes=64)
         nc.vector.tensor_copy(out=picked[:], in_=scales[:].bitcast(U8).indirect(offsets[:]))
-        first, second, whole = slice(0, GATHERS[0]), slice(GATHERS[0], N), slice(0, N)
-        moves = [(r, first) for r in range(3)] + [(3, whole)] + [(r, second) for r in range(3)]
+        first, second, third = [slice(s0, s0 + width) for s0, width in runs(GATHERS)]
+        moves = [(r, first) for r in range(3)] + [(3, slice(0, N))]
+        moves = moves + [(0, second), (1, second), (2, slice(second.start, N)), (0, third), (1, third)]
         for r, slots in moves:
             rows = picked[ROW0 + ROW_STEP * r : ROW0 + 16 * ROW_STEP : 4 * ROW_STEP, slots]
             nc.scalar.dma_start(out=key_scales[r:P:32, slots.start // 4 : slots.stop // 4], in_=rows.bitcast(I32))
@@ -80,7 +81,7 @@ def tile_attend_page_margin_kernel(tc, qT, k_words, k_scales, th, offs, out):
 
         gathered = []
         for h, (s0, width) in enumerate(runs(GATHERS)):
-            kw = pool.tile([P, width], U32, name=f"key_words{h}", align_bytes=64)
+            kw = pool.tile([P, width], U32, name=f"key_words{h}", tag=f"key_words{h}", align_bytes=64)
             nc.vector.tensor_copy(out=kw[:], in_=words[:].bitcast(U32).indirect(offsets[:, s0 // 16 : (s0 + width) // 16]))
             gathered.append((s0, width, kw))
 
@@ -104,7 +105,7 @@ def tile_attend_page_margin_kernel(tc, qT, k_words, k_scales, th, offs, out):
                 op=ALU.max,
             )
 
-        denom = pool.tile([P, PAGES], F32, name="denom")
+        denom = pool.tile([P, PAGES], F32, name="denom", tag=f"key_words{len(GATHERS) - 1}", align_bytes=64)
         inv = pool.tile([P, PAGES], F32, name="inv")
         margin = pool.tile([P, PAGES], F32, name="margin")
         res = pool.tile([P, PAGES], F32, name="res")

from contextlib import ExitStack

import concourse.mybir as mybir

F32 = mybir.dt.float32
BF16 = mybir.dt.bfloat16
I32 = mybir.dt.int32
U32 = mybir.dt.uint32
U16 = mybir.dt.uint16
U8 = mybir.dt.uint8
FP8X4 = mybir.dt.float8_e4m3fn_x4
ALU = mybir.AluOpType

P = 128
PACK = 4
T = 4096
N = 1024
NQ = 128
SEG = 32
PAGES = N // SEG
GATHERS = (384, 384, 256,)
PASSES = (128, 128, 128, 128, 128, 128, 128, 128,)
PARTS = (24, 4, 4,)
ROW0 = 11
ROW_STEP = 7

FLOPS = 2 * 512 * NQ * N


def runs(widths):
    starts = [sum(widths[:i]) for i in range(len(widths))]
    return list(zip(starts, widths))


def tile_attend_page_margin_kernel(tc, qT, k_words, k_scales, th, offs, out):
    nc = tc.nc
    with ExitStack() as ctx:
        pool = ctx.enter_context(tc.tile_pool(name="held", bufs=1))
        psum = ctx.enter_context(tc.psum_pool(name="psum", bufs=1))

        offsets = pool.tile([P, N // 16], U16, name="offsets")
        scales = pool.tile([P, T // 4], I32, name="scales", align_bytes=64)
        key_scales = pool.tile([P, N // 4], I32, name="key_scales", align_bytes=64)
        words = pool.tile([P, T], I32, name="words", align_bytes=64)
        q_raw = pool.tile([P, PACK, NQ], F32, name="q_raw", align_bytes=64)
        th_rows = pool.tile([P, 32], F32, name="th_rows", align_bytes=64)

        nc.vector.memset(scales[:], 0)
        nc.vector.memset(key_scales[:], 0)

        nc.sync.dma_start(out=q_raw[:], in_=qT[0].rearrange("(p j) w -> p j w", j=PACK))
        nc.sync.dma_start(offsets[:], offs)
        nc.sync.dma_start(out=th_rows[31:P:32, :], in_=th[0].rearrange("(g i) o -> g (i o)", i=32))
        nc.sync.dma_start(out=scales[ROW0 : ROW0 + 16 * ROW_STEP : ROW_STEP, :], in_=k_scales[0].bitcast(I32))
        nc.sync.dma_start(out=words[:], in_=k_words[0].rearrange("p n t -> p (n t)").bitcast(I32))
        for g in range(4):
            nc.vector.memset(th_rows[32 * g : 32 * g + 31, :], 0.0)

        q_bf = pool.tile([P, NQ, PACK], BF16, name="q_bf", align_bytes=64)
        nc.vector.tensor_copy(
            out=q_bf[:].rearrange("p (c i) j -> p c j i", i=PACK), in_=q_raw[:].rearrange("p j (c i) -> p c j i", i=PACK)
        )

        picked = pool.tile([P, N], U8, name="picked", align_bytes=64)
        nc.vector.tensor_copy(out=picked[:], in_=scales[:].bitcast(U8).indirect(offsets[:]))
        first, second, third = [slice(s0, s0 + width) for s0, width in runs(GATHERS)]
        moves = [(r, first) for r in range(3)] + [(3, slice(0, N))]
        moves = moves + [(0, second), (1, second), (2, slice(second.start, N)), (0, third), (1, third)]
        for r, slots in moves:
            rows = picked[ROW0 + ROW_STEP * r : ROW0 + 16 * ROW_STEP : 4 * ROW_STEP, slots]
            nc.scalar.dma_start(out=key_scales[r:P:32, slots.start // 4 : slots.stop // 4], in_=rows.bitcast(I32))

        q_codes = pool.tile([P, NQ], U32, name="q_codes", align_bytes=64)
        q_scales = pool.tile([P, NQ], U8, name="q_scales", align_bytes=64)
        nc.vector.quantize_mx(out=q_codes[:].bitcast(FP8X4), scales=q_scales[:], in_=q_bf[:].rearrange("p w j -> p (w j)"))

        th_cols = pool.tile([P, 32], F32, name="th_cols", align_bytes=64)
        nc.vector.transpose(out=th_cols[:], in_=th_rows[:])
        one_less_thr = pool.tile([P, 1], F32, name="one_less_thr")
        nc.vector.tensor_scalar(out=one_less_thr[:], in0=th_cols[:, 31:32], scalar1=-1.0, scalar2=1.0, op0=ALU.mult, op1=ALU.add)

        gathered = []
        for h, (s0, width) in enumerate(runs(GATHERS)):
            kw = pool.tile([P, width], U32, name=f"key_words{h}", tag=f"key_words{h}", align_bytes=64)
            nc.vector.tensor_copy(out=kw[:], in_=words[:].bitcast(U32).indirect(offsets[:, s0 // 16 : (s0 + width) // 16]))
            gathered.append((s0, width, kw))

        best = pool.tile([P, PAGES], F32, name="best")
        for m, (s0, width) in enumerate(runs(PASSES)):
            g0, kw = [(g0, kw) for g0, gw, kw in gathered if g0 <= s0 < g0 + gw][0]
            scores = psum.tile([P, 512], F32, name=f"scores{m}")
            nc.tensor.matmul_mx(
                out=scores[:, 0:width],
                lhsT=q_codes[:].bitcast(FP8X4),
                lhsT_scale=q_scales[:],
                rhs=kw[:, s0 - g0 : s0 - g0 + width].bitcast(FP8X4),
                rhs_scale=key_scales[:].bitcast(U8)[:, s0 : s0 + width],
                start=True,
                stop=True,
            )
            nc.vector.tensor_reduce(
                out=best[:, s0 // SEG : (s0 + width) // SEG],
                in_=scores[:, 0:width].rearrange("p (j s) -> p j s", s=SEG),
                axis=mybir.AxisListType.X,
                op=ALU.max,
            )

        denom = pool.tile([P, PAGES], F32, name="denom", tag=f"key_words{len(GATHERS) - 1}", align_bytes=64)
        inv = pool.tile([P, PAGES], F32, name="inv")
        margin = pool.tile([P, PAGES], F32, name="margin")
        res = pool.tile([P, PAGES], F32, name="res")
        parts = [slice(j0, j0 + n) for j0, n in runs(PARTS)]
        for c in parts:
            nc.vector.tensor_scalar(out=denom[:, c], in0=best[:, c], scalar1=one_less_thr[:], scalar2=1.0, op0=ALU.add, op1=ALU.max)
        for c in parts:
            nc.vector.reciprocal(out=inv[:, c], in_=denom[:, c])
        nc.vector.tensor_scalar(out=margin[:], in0=best[:], scalar1=th_cols[:, 31:32], scalar2=0.0, op0=ALU.subtract, op1=ALU.max)
        for c in parts:
            nc.vector.tensor_tensor(out=res[:, c], in0=margin[:, c], in1=inv[:, c], op=ALU.mult)
        nc.sync.dma_start(out=out[0], in_=res[:])
